import numpy as np
import ml_dtypes


def mxq(x, axis, fmt="e4m3"):
    dtype, down = {"e4m3": (ml_dtypes.float8_e4m3fn, 7), "e5m2": (ml_dtypes.float8_e5m2, 14)}[fmt]
    v = np.moveaxis(np.asarray(x, np.float32).astype(ml_dtypes.bfloat16).astype(np.float64), axis, -1)
    blocks = v.reshape(v.shape[:-1] + (-1, 32))
    amax = np.abs(blocks).max(-1, keepdims=True)
    byte = np.maximum(np.where(amax > 0, np.frexp(amax)[1] - 1 + 127, 0) - down, 1)
    scale = np.exp2(byte - 127.0)
    codes = (blocks / scale).astype(np.float32).astype(dtype).astype(np.float64)
    return np.moveaxis((codes * scale).reshape(v.shape), -1, axis)


WIDE = False


def mx_kscale(k):
    if not WIDE:
        return np.ones(k)
    levels = np.array([10, -10, 5, -5, 0])
    if k % 512:
        return np.exp2(np.random.permutation(np.resize(levels, k // 32))).repeat(32)
    a = np.empty((k // 512, 16))
    for p in range(k // 512):
        a[p, :8] = np.random.permutation(np.resize(levels, 8))
        for g in range(8):
            far = levels[np.abs(levels - a[p, g]) >= 10]
            a[p, g + 8] = far[np.random.randint(len(far))]
    return np.exp2(a.ravel()).repeat(32)


BF16 = ml_dtypes.bfloat16


def bf(x):
    return np.asarray(x, np.float32).astype(BF16)


def f64(x):
    return np.asarray(x).astype(np.float64)


E2M1 = np.array([0.0, 0.5, 1.0, 1.5, 2.0, 3.0, 4.0, 6.0, -0.0, -0.5, -1.0, -1.5, -2.0, -3.0, -4.0, -6.0])


def pack_weight(w, fmt):
    k, n = w.shape
    w = f64(bf(w)).reshape(k // 32, 32, n)
    amax = np.abs(w).max(1)
    if fmt == "e4m3":
        byte = np.frexp(amax)[1] - 1 + 127 - 7
    else:
        mant, ex = np.frexp(amax / 6.0)
        byte = np.where(mant > 0.5, ex, ex - 1) + 127
    byte = np.clip(np.where(amax > 0, byte, 1), 1, 254)
    scaled = (w * np.exp2(127.0 - byte)[:, None, :]).reshape(k, n).astype(np.float32)
    by_word = np.ascontiguousarray(scaled.reshape(k // 512, 128, 4, n).transpose(0, 1, 3, 2))
    if fmt == "e4m3":
        words = by_word.astype(ml_dtypes.float8_e4m3fn).view(np.uint8)
    else:
        c = by_word.astype(ml_dtypes.float4_e2m1fn).view(np.uint8) & 0xF
        words = c[..., 0::2] | (c[..., 1::2] << 4)
    return np.ascontiguousarray(words), np.ascontiguousarray(byte.astype(np.uint8).reshape(k // 512, 16, n))


def unpack_weight(words, scales, fmt):
    g, p, n, _ = words.shape
    if fmt == "e4m3":
        vals = np.ascontiguousarray(words).view(ml_dtypes.float8_e4m3fn).astype(np.float64)
    else:
        nib = np.empty((g, p, n, 4), np.uint8)
        nib[..., 0::2] = words & 0xF
        nib[..., 1::2] = words >> 4
        vals = E2M1[nib]
    vals = vals * np.repeat(np.exp2(scales.astype(np.float64) - 127.0), 8, axis=1)[..., None]
    return vals.transpose(0, 1, 3, 2).reshape(g * 512, n)

E4M3FN = np.array([(-1.0 if i & 128 else 1.0) * ((1.0 + (i & 7) / 8.0) * 2.0 ** (((i >> 3) & 15) - 7) if i & 120 else (i & 7) * 2.0 ** -9) for i in range(256)])


def e4m3fn_bytes(y):
    return np.clip(np.asarray(y, np.float64), -448.0, 448.0).astype(np.float32).astype(ml_dtypes.float8_e4m3fn).view(np.uint8)


def e4m3fn_values(b):
    return E4M3FN[b]


B, H, T, S, E = 2, 2, 512, 1024, 512
D = H * E
EPS = 1e-5


def draw0():
    s, t, r = mx_kscale(E), mx_kscale(S), mx_kscale(D)
    q = np.random.standard_normal((B, H, T, E)) * s
    k = np.random.standard_normal((B, H, S, E)) / s
    rab = 0.8 * np.random.standard_normal((H, T, S))
    c = (1.0 + 0.1 * np.random.standard_normal(S)) * t
    v = np.random.standard_normal((B, H, S, E)) + 0.5 * np.random.standard_normal((B, H, S, 1))
    v = v * (0.02 / np.sqrt(S)) / t[:, None]
    x = np.random.standard_normal((B, T, D)) * r
    wu = np.random.standard_normal((D, D)) / np.sqrt(D) / r[:, None]
    wu_words, wu_scales = pack_weight(wu, "e4m3")
    return {"q": bf(q), "k": bf(k), "rab": bf(rab), "c": bf(c), "v": bf(v), "x": bf(x), "wu_words": wu_words, "wu_scales": wu_scales}


def sigmoid(z):
    return 1.0 / (1.0 + np.exp(-z))


def silu_gate(z):
    return z * sigmoid(z)


def plain_layer_norm(p):
    mean = np.mean(p, axis=-1, keepdims=True)
    centered = p - mean
    var = np.mean(centered * centered, axis=-1, keepdims=True)
    return centered / np.sqrt(var + EPS)


def core(q, k, rab, c, v, x, wu_words, wu_scales):
    b, h, t, e = q.shape
    qq = mxq(f64(q), 3, "e4m3")
    kq = mxq(f64(k), 3, "e4m3")
    l = (qq @ kq.transpose(0, 1, 3, 2)) / np.sqrt(e) + f64(rab)[None, :, :, :]
    a = f64(c)[None, None, None, :] * l * sigmoid(l)
    o = mxq(a, 3, "e4m3") @ mxq(f64(v), 2, "e4m3")
    p = np.transpose(o, (0, 2, 1, 3)).reshape(b, t, h * e)
    n = plain_layer_norm(p)
    u = silu_gate(mxq(f64(x), 2, "e4m3") @ unpack_weight(wu_words, wu_scales, "e4m3"))
    return n * u


def setup_inputs():
    drawn = draw0()
    full = np.asarray(drawn['v']).astype(np.float64)
    scale = (np.abs(full).reshape(2, 2, 1024, 4, 128).max(axis=(4,)) / 448.0).astype(np.float32)
    given = {}
    for key, value in drawn.items():
        if key == 'v':
            given['v_bytes'] = e4m3fn_bytes(full / np.repeat(scale.astype(np.float64), 128, axis=3))
            given['v_scale'] = scale
        else:
            given[key] = value
    return given


def reference(q, k, rab, c, v_bytes, v_scale, x, wu_words, wu_scales):
    return core(q, k, rab, c, e4m3fn_values(v_bytes) * np.repeat(v_scale.astype(np.float64), 128, axis=3), x, wu_words, wu_scales)

@@ -1,0 +1,308 @@
+from contextlib import ExitStack
+
+import concourse.mybir as mybir
+from concourse.masks import make_identity
+
+B, H, T, S, E = 2, 2, 512, 1024, 512
+D = H * E
+EPS = 1e-5
+FLOPS = 2 * (2 * B * H * T * S * E + B * T * D * D)
+
+F32 = mybir.dt.float32
+BF16 = mybir.dt.bfloat16
+U32 = mybir.dt.uint32
+I32 = mybir.dt.int32
+U8 = mybir.dt.uint8
+FP8 = mybir.dt.float8_e4m3fn
+FP8X4 = mybir.dt.float8_e4m3fn_x4
+ALU = mybir.AluOpType
+ACT = mybir.ActivationFunctionType
+
+P = 128
+GS = S // 512
+GD = D // 512
+NT = T // P
+ISQ = 1.0 / (E ** 0.5)
+
+
+def tile_hstupointwisetransducer_d1p_kernel(tc, q, k, rab, c, v_bytes, v_scale, x, wu_words, wu_scales, out):
+    nc = tc.nc
+    with ExitStack() as ctx:
+        const = ctx.enter_context(tc.tile_pool(name="const", bufs=1))
+        codes = ctx.enter_context(tc.tile_pool(name="codes", bufs=1))
+        raw = ctx.enter_context(tc.tile_pool(name="raw", bufs=4))
+        work = ctx.enter_context(tc.tile_pool(name="work", bufs=3))
+        ps_tr = ctx.enter_context(tc.psum_pool(name="ps_tr", bufs=2))
+        ps_sc = ctx.enter_context(tc.psum_pool(name="ps_sc", bufs=2))
+        ps_acc = ctx.enter_context(tc.psum_pool(name="ps_acc", bufs=4))
+
+        ident = const.tile([P, P], F32)
+        make_identity(nc, ident[:])
+        neghalf = const.tile([P, 1], F32)
+        nc.gpsimd.memset(neghalf[:], -0.5)
+        warm = const.tile([P, 1], F32)
+        nc.scalar.activation(out=warm[:], in_=neghalf[:], func=ACT.Silu)
+        wsc = const.tile([P, D], U8, align_bytes=64)
+        nc.gpsimd.memset(wsc[:].bitcast(I32), 0)
+
+        vs = const.tile([P, B * H * GS, 16], F32)
+        nc.scalar.dma_start(out=vs[:], in_=v_scale.rearrange("b h (g p t) c -> p (b h g) (t c)", p=P, t=4))
+        gain = const.tile([P, GS, 4], BF16)
+        nc.scalar.dma_start(out=gain[:], in_=c.rearrange("(g p t) -> p g t", p=P, t=4))
+
+        def load_v(b, h):
+            vb = raw.tile([P, GS, 4 * E], U8, name="vb", bufs=3)
+            nc.sync.dma_start(out=vb[:], in_=v_bytes[b, h].rearrange("(g p t) f -> p g (t f)", p=P, t=4))
+            return vb
+
+        def load_k(b, h, g):
+            kr = raw.tile([P, 4, E], BF16, name="kr", bufs=4)
+            nc.sync.dma_start(out=kr[:], in_=k[b, h].rearrange("(g m t) e -> g m t e", m=P, t=4)[g])
+            return kr
+
+        def load_q(b, h):
+            qr = raw.tile([P, NT, E], BF16, name="qr", bufs=2)
+            nc.sync.dma_start(out=qr[:], in_=q[b, h].rearrange("(m n) e -> m n e", n=NT))
+            return qr
+
+        def load_rab(h, n):
+            rr = raw.tile([P, S], BF16, name="rr", bufs=4)
+            nc.sync.dma_start(out=rr[:], in_=rab[h].rearrange("(m n) s -> m n s", n=NT)[:, n])
+            return rr
+
+        def load_x(b):
+            xr = raw.tile([P, NT, D], BF16, name="xr", bufs=1)
+            nc.sync.dma_start(out=xr[:], in_=x[b].rearrange("(m n) d -> m n d", n=NT))
+            return xr
+
+        def turn(srcs, dst, use_scalar):
+            bank = ps_tr.tile([P, 4, P], F32, name="bank")
+            for i in range(2):
+                for u in range(2):
+                    nc.tensor.transpose(out=bank[:, 2 * i + u, :], in_=srcs[i][:, u::2], identity=ident[:])
+            o = dst.rearrange("p c t -> p (c t)").bitcast(F32).rearrange("p (i m u) -> p i m u", i=2, u=2)
+            s = bank[:].rearrange("p (i u) m -> p i m u", u=2)
+            if use_scalar:
+                nc.scalar.copy(out=o, in_=s)
+            else:
+                nc.vector.tensor_copy(out=o, in_=s)
+
+        def quantize(cd, sc, grp):
+            nc.vector.quantize_mx(out=cd.bitcast(FP8X4), scales=sc, in_=grp)
+
+        def words(ap):
+            return ap.bitcast(F32)
+
+        kc, ks, qc, qs, vc, vsc, xc, xs = {}, {}, {}, {}, {}, {}, {}, {}
+        rabt = {}
+        for h in range(H):
+            rabt[h] = codes.tile([P, NT, GS, P, 4], BF16, name=f"rabt{h}", align_bytes=64)
+        for b in range(B):
+            xc[b] = codes.tile([P, GD, T], U32, name=f"xc{b}", align_bytes=64)
+            xs[b] = codes.tile([P, GD, T], U8, name=f"xs{b}", align_bytes=64)
+            for h in range(H):
+                kc[b, h] = codes.tile([P, S], U32, name=f"kc{b}{h}", align_bytes=64)
+                ks[b, h] = codes.tile([P, S], U8, name=f"ks{b}{h}", align_bytes=64)
+                qc[b, h] = codes.tile([P, T], U32, name=f"qc{b}{h}", align_bytes=64)
+                qs[b, h] = codes.tile([P, T], U8, name=f"qs{b}{h}", align_bytes=64)
+                vc[b, h] = codes.tile([P, GS, E], U32, name=f"vc{b}{h}", align_bytes=64)
+                vsc[b, h] = codes.tile([P, GS, E], U8, name=f"vsc{b}{h}", align_bytes=64)
+        ww = codes.tile([P, GD, D], U32, name="ww", align_bytes=64)
+
+        def prep_v(b, h, vb):
+            for g in range(GS):
+                grp = work.tile([P, 512, 4], BF16, name="grp", align_bytes=64, bufs=5)
+                wide = work.tile([P, 4, E], BF16, name="wide", bufs=2)
+                for t in range(4):
+                    for j in range(4):
+                        nc.scalar.activation(
+                            out=wide[:, t, P * j : P * (j + 1)], in_=vb[:, g, E * t + P * j : E * t + P * (j + 1)].bitcast(FP8),
+                            func=ACT.Copy, scale=vs[:, (b * H + h) * GS + g, 4 * t + j : 4 * t + j + 1],
+                        )
+                nc.vector.tensor_copy(
+                    out=grp[:].rearrange("p (f i) t -> p f t i", i=4), in_=wide[:].rearrange("p t (f i) -> p f t i", i=4)
+                )
+                quantize(vc[b, h][:, g, :], vsc[b, h][:, g, :], grp[:].rearrange("p c t -> p (c t)"))
+
+        def prep_k(b, h, g, kr):
+            grp = work.tile([P, 512, 4], BF16, name="grp", align_bytes=64, bufs=5)
+            w = words(kr[:])
+            for i in range(2):
+                turn([w[:, 2 * i, :], w[:, 2 * i + 1, :]], grp[:, 256 * i : 256 * (i + 1), :], True)
+            sl = slice(512 * g, 512 * (g + 1))
+            quantize(kc[b, h][:, sl], ks[b, h][:, sl], grp[:].rearrange("p c t -> p (c t)"))
+
+        def prep_q(b, h, qr):
+            grp = work.tile([P, 512, 4], BF16, name="grp", align_bytes=64, bufs=5)
+            w = words(qr[:])
+            for i in range(2):
+                turn([w[:, 2 * i, :], w[:, 2 * i + 1, :]], grp[:, 256 * i : 256 * (i + 1), :], True)
+            quantize(qc[b, h][:], qs[b, h][:], grp[:].rearrange("p c t -> p (c t)"))
+
+        def prep_x(b, g, xr):
+            grp = work.tile([P, 512, 4], BF16, name="grp", align_bytes=64, bufs=5)
+            w = words(xr[:])
+            for i in range(2):
+                turn([w[:, n, 256 * g : 256 * (g + 1)] for n in (2 * i, 2 * i + 1)], grp[:, 256 * i : 256 * (i + 1), :], True)
+            quantize(xc[b][:, g, :], xs[b][:, g, :], grp[:].rearrange("p c t -> p (c t)"))
+
+        def prep_rab(h, n, rr):
+            w = words(rr[:])
+            turn([w[:, 256 * g : 256 * (g + 1)] for g in range(GS)], rabt[h][:, n].rearrange("p g m t -> p (g m) t"), h == 1)
+
+        def scores(b, h, n):
+            banks = []
+            for g in range(GS):
+                sc = ps_sc.tile([P, 4, P], F32, name="sc")
+                for t in range(4):
+                    c0 = 512 * g + P * t
+                    nc.tensor.matmul_mx(
+                        out=sc[:, t, :],
+                        lhsT=kc[b, h][:, c0 : c0 + P].bitcast(FP8X4),
+                        lhsT_scale=ks[b, h][:, c0 : c0 + P],
+                        rhs=qc[b, h][:, P * n : P * (n + 1)].bitcast(FP8X4),
+                        rhs_scale=qs[b, h][:, P * n : P * (n + 1)],
+                        start=True,
+                        stop=True,
+                    )
+                banks.append(sc)
+            return banks
+
+        def logits(b, h, n):
+            banks = scores(b, h, n)
+            l = work.tile([P, GS, P, 4], F32, name="l", bufs=2)
+            for g in range(GS):
+                nc.vector.scalar_tensor_tensor(
+                    out=l[:, g], in0=banks[g][:].rearrange("p t m -> p m t"), scalar=ISQ, in1=rabt[h][:, n, g],
+                    op0=ALU.mult, op1=ALU.add,
+                )
+            s = work.tile([P, GS, P, 4], F32, name="s", bufs=3)
+            nc.scalar.activation(out=s[:], in_=l[:], func=ACT.Silu)
+            return s
+
+        def weights(b, h, n, s):
+            a = work.tile([P, GS, P, 4], BF16, name="a", align_bytes=64, bufs=3)
+            eng = nc.gpsimd if (h == 0 and n % 2 == 1) or (h == 1 and n == 1) else nc.vector
+            eng.tensor_tensor(out=a[:], in0=s[:], in1=gain[:].unsqueeze(2).to_broadcast([P, GS, P, 4]), op=ALU.mult)
+            ac = work.tile([P, GS * P], U32, name=f"ac{h}", align_bytes=64, bufs=5 - 2 * h)
+            asc = work.tile([P, GS * P], U8, name=f"asc{h}", align_bytes=64, bufs=5 - 2 * h)
+            quantize(ac[:], asc[:], a[:].rearrange("p g m t -> p (g m t)"))
+            made[b, h, n] = (ac, asc)
+
+        def values(b, h, ac, asc):
+            o = ps_acc.tile([P, E], F32, name="acc")
+            for g in range(GS):
+                nc.tensor.matmul_mx(
+                    out=o[:],
+                    lhsT=ac[:, P * g : P * (g + 1)].bitcast(FP8X4),
+                    lhsT_scale=asc[:, P * g : P * (g + 1)],
+                    rhs=vc[b, h][:, g, :].bitcast(FP8X4),
+                    rhs_scale=vsc[b, h][:, g, :],
+                    start=(g == 0),
+                    stop=(g == GS - 1),
+                )
+            return o
+
+        def gate(b, n):
+            u = work.tile([P, D], F32, name="u", bufs=3)
+            for f in range(2):
+                acc = ps_acc.tile([P, E], F32, name="acc")
+                cols = slice(E * f, E * (f + 1))
+                for g in range(GD):
+                    nc.tensor.matmul_mx(
+                        out=acc[:],
+                        lhsT=xc[b][:, g, P * n : P * (n + 1)].bitcast(FP8X4),
+                        lhsT_scale=xs[b][:, g, P * n : P * (n + 1)],
+                        rhs=ww[:, g, cols].bitcast(FP8X4),
+                        rhs_scale=wsc[4 * g : P, cols],
+                        start=(g == 0),
+                        stop=(g == GD - 1),
+                    )
+                nc.scalar.activation(out=u[:, cols], in_=acc[:], func=ACT.Silu)
+            return u
+
+        def finish(b, n, outs, u):
+            st = work.tile([P, 2, 6], F32, name="st", bufs=3)
+            for h in range(H):
+                nc.vector.bn_stats(out=st[:, h, :], in_=outs[h][:])
+            mv = work.tile([P, 2], F32, name="mv", bufs=3)
+            nc.vector.bn_aggr(out=mv[:], in_=st[:].rearrange("p h s -> p (h s)"))
+            ve = work.tile([P, 1], F32, name="ve", bufs=3)
+            nc.gpsimd.tensor_scalar(out=ve[:], in0=mv[:, 1:2], scalar1=1.0, scalar2=EPS, op0=ALU.mult, op1=ALU.add)
+            rs = work.tile([P, 1], F32, name="rs", bufs=3)
+            nc.gpsimd.tensor_tensor(out=rs[:], in0=ve[:], in1=neghalf[:], op=ALU.pow)
+            y = work.tile([P, D], F32, name="y", bufs=2)
+            for h in range(H):
+                cols = slice(E * h, E * (h + 1))
+                nc.vector.scalar_tensor_tensor(
+                    out=y[:, cols], in0=outs[h][:], scalar=mv[:, 0:1], in1=u[:, cols], op0=ALU.subtract, op1=ALU.mult
+                )
+            z = work.tile([P, D], F32, name="z", bufs=2)
+            nc.gpsimd.tensor_scalar(out=z[:], in0=y[:], scalar1=rs[:], scalar2=0.0, op0=ALU.mult, op1=ALU.add)
+            nc.sync.dma_start(out=out[b].rearrange("(m n) d -> m n d", n=NT)[:, n], in_=z[:])
+
+        made = {}
+
+        def load_w():
+            nc.sync.dma_start(
+                out=ww[:].bitcast(I32),
+                in_=wu_words.rearrange("g p n t -> g p (n t)").bitcast(I32).rearrange("g p n -> p g n"),
+            )
+            for qd in range(4):
+                nc.sync.dma_start(
+                    out=wsc[32 * qd : 32 * qd + 8, :].bitcast(I32), in_=wu_scales[:, 4 * qd : 4 * qd + 4, :].bitcast(I32)
+                )
+
+        steps = {0: [], 1: []}
+        for b in range(B):
+            for h in range(H):
+                steps[b].append(("vb", lambda b=b, h=h: load_v(b, h), lambda r, b=b, h=h: prep_v(b, h, r)))
+                for g in range(GS):
+                    steps[b].append(("kr", lambda b=b, h=h, g=g: load_k(b, h, g), lambda r, b=b, h=h, g=g: prep_k(b, h, g, r)))
+                steps[b].append(("qr", lambda b=b, h=h: load_q(b, h), lambda r, b=b, h=h: prep_q(b, h, r)))
+                if b == 0:
+                    for n in range(NT):
+                        steps[b].append(("rr", lambda h=h, n=n: load_rab(h, n), lambda r, h=h, n=n: prep_rab(h, n, r)))
+            steps[b].append(("xr", lambda b=b: load_x(b), lambda r, b=b: [prep_x(b, gg, r) for gg in range(GD)]))
+        order = steps[0] + steps[1]
+        room = {"vb": 3, "kr": 4, "qr": 2, "rr": 4, "xr": 1}
+        state = {"loaded": 0, "done": 0}
+        tiles = {}
+
+        def load_ahead():
+            while state["loaded"] < len(order) and room[order[state["loaded"]][0]] > 0:
+                kind, load, prep = order[state["loaded"]]
+                room[kind] -= 1
+                tiles[state["loaded"]] = load()
+                if state["loaded"] == len(steps[0]) - 1:
+                    load_w()
+                state["loaded"] += 1
+
+        def prepare(count):
+            for i in range(count):
+                if state["done"] < len(order):
+                    load_ahead()
+                    kind, load, prep = order[state["done"]]
+                    prep(tiles[state["done"]])
+                    room[kind] += 1
+                    state["done"] += 1
+            load_ahead()
+
+        def close(b, n):
+            finish(b, n, [values(b, h, *made[b, h, n]) for h in range(H)], gate(b, n))
+
+        units = [(b, h, n) for b in range(B) for h in range(H) for n in range(NT)]
+        ahead = {(0, 0): [3, 2, 2, 2], (0, 1): [1, 1, 1, 1], (1, 0): [2, 1, 1, 1], (1, 1): [0, 0, 0, 0]}
+        prepare(8)
+        held = {}
+        for i in range(len(units) + 1):
+            if i < len(units):
+                held[units[i]] = logits(*units[i])
+            if i > 0:
+                b, h, n = units[i - 1]
+                weights(b, h, n, held[b, h, n])
+                if h == 1:
+                    close(b, n)
+            if i < len(units):
+                b, h, n = units[i]
+                prepare(ahead[b, h][n])

@@ -17,12 +17,72 @@ FP8 = mybir.dt.float8_e4m3fn
 FP8X4 = mybir.dt.float8_e4m3fn_x4
 ALU = mybir.AluOpType
 ACT = mybir.ActivationFunctionType
+ENG = mybir.EngineType
 
 P = 128
 GS = S // 512
 GD = D // 512
 NT = T // P
 ISQ = 1.0 / (E ** 0.5)
+
+
+def k_jobs(b, h):
+    return [("k", b, h, g, i) for g in range(GS) for i in range(2)]
+
+
+def q_jobs(b, h):
+    return [("q", b, h, i) for i in range(2)]
+
+
+def x_jobs(b):
+    return [("x", b, g, i) for g in range(GD) for i in range(2)]
+
+
+def w_jobs(b, h):
+    return [(b, h, g, i) for g in range(GS) for i in range(2)]
+
+
+K01, Q01, X0, K10, Q10, K11, Q11, X1 = (
+    k_jobs(0, 1), q_jobs(0, 1), x_jobs(0), k_jobs(1, 0), q_jobs(1, 0), k_jobs(1, 1), q_jobs(1, 1), x_jobs(1)
+)
+W00, W01, W10, W11 = w_jobs(0, 0), w_jobs(0, 1), w_jobs(1, 0), w_jobs(1, 1)
+
+TURN = {
+    0: [("r", 0, 1)] + K01[0:2],
+    1: [("r", 0, 2)] + K01[2:4],
+    2: [("r", 0, 3)] + Q01,
+    3: [("r", 1, 0)] + X0[0:2],
+    4: [("r", 1, 1)] + X0[2:4],
+    5: [("r", 1, 2)] + K10[0:3],
+    6: [("r", 1, 3)] + K10[3:4] + Q10,
+    7: K11[0:1],
+    8: K11[1:2],
+    9: K11[2:4],
+    10: Q11,
+    11: X1[0:2],
+    12: X1[2:4],
+}
+WIDEN = {
+    0: W00[0:1], 1: W00[1:2], 2: W00[2:4], 3: W01[0:2], 4: W01[2:4],
+    7: W10[0:1], 8: W10[1:2], 9: W10[2:3], 10: W10[3:4], 11: W11[0:2], 12: W11[2:4],
+}
+MERGE = {2: [(0, 0, 0)], 3: [(0, 0, 1)], 4: [(0, 1, 0)], 5: [(0, 1, 1)], 10: [(1, 0, 0)], 11: [(1, 0, 1)], 12: [(1, 1, 0)], 13: [(1, 1, 1)]}
+EARLY = {3: [("q", 0, 1)], 5: [("x", 0, 1)], 13: [("x", 1, 1)], 7: [("k", 1, 0, 1), ("q", 1, 0)], 11: [("q", 1, 1)]}
+LATE = {
+    1: [("k", 0, 1, 0)],
+    2: [("k", 0, 1, 1)],
+    3: [("v", 0, 0, 0)],
+    4: [("v", 0, 0, 1), ("x", 0, 0)],
+    5: [("v", 0, 1, 0), ("v", 0, 1, 1)],
+    6: [("k", 1, 0, 0)],
+    9: [("k", 1, 1, 0)],
+    10: [("k", 1, 1, 1)],
+    11: [("v", 1, 0, 0)],
+    12: [("v", 1, 0, 1), ("x", 1, 0)],
+    13: [("v", 1, 1, 0), ("v", 1, 1, 1)],
+}
+GATE = {5: [(0, 0)], 6: [(0, 1)], 7: [(0, 2)], 8: [(0, 3)], 13: [(1, 0)], 14: [(1, 1)], 15: [(1, 2), (1, 3)]}
+GAIN_ON_POOL = ()
 
 
 def tile_hstupointwisetransducer_d1p_kernel(tc, q, k, rab, c, v_bytes, v_scale, x, wu_words, wu_scales, out):
@@ -34,67 +94,18 @@ def tile_hstupointwisetransducer_d1p_kernel(tc, q, k, rab, c, v_bytes, v_scale, 
         work = ctx.enter_context(tc.tile_pool(name="work", bufs=3))
         ps_tr = ctx.enter_context(tc.psum_pool(name="ps_tr", bufs=2))
         ps_sc = ctx.enter_context(tc.psum_pool(name="ps_sc", bufs=2))
-        ps_acc = ctx.enter_context(tc.psum_pool(name="ps_acc", bufs=4))
-
-        ident = const.tile([P, P], F32)
-        make_identity(nc, ident[:])
-        neghalf = const.tile([P, 1], F32)
-        nc.gpsimd.memset(neghalf[:], -0.5)
-        warm = const.tile([P, 1], F32)
-        nc.scalar.activation(out=warm[:], in_=neghalf[:], func=ACT.Silu)
-        wsc = const.tile([P, D], U8, align_bytes=64)
-        nc.gpsimd.memset(wsc[:].bitcast(I32), 0)
+        ps_o = ctx.enter_context(tc.psum_pool(name="ps_o", bufs=2))
+        ps_ga = ctx.enter_context(tc.psum_pool(name="ps_ga", bufs=2))
 
         vs = const.tile([P, B * H * GS, 16], F32)
-        nc.scalar.dma_start(out=vs[:], in_=v_scale.rearrange("b h (g p t) c -> p (b h g) (t c)", p=P, t=4))
         gain = const.tile([P, GS, 4], BF16)
-        nc.scalar.dma_start(out=gain[:], in_=c.rearrange("(g p t) -> p g t", p=P, t=4))
-
-        def load_v(b, h):
-            vb = raw.tile([P, GS, 4 * E], U8, name="vb", bufs=3)
-            nc.sync.dma_start(out=vb[:], in_=v_bytes[b, h].rearrange("(g p t) f -> p g (t f)", p=P, t=4))
-            return vb
-
-        def load_k(b, h, g):
-            kr = raw.tile([P, 4, E], BF16, name="kr", bufs=4)
-            nc.sync.dma_start(out=kr[:], in_=k[b, h].rearrange("(g m t) e -> g m t e", m=P, t=4)[g])
-            return kr
-
-        def load_q(b, h):
-            qr = raw.tile([P, NT, E], BF16, name="qr", bufs=2)
-            nc.sync.dma_start(out=qr[:], in_=q[b, h].rearrange("(m n) e -> m n e", n=NT))
-            return qr
-
-        def load_rab(h, n):
-            rr = raw.tile([P, S], BF16, name="rr", bufs=4)
-            nc.sync.dma_start(out=rr[:], in_=rab[h].rearrange("(m n) s -> m n s", n=NT)[:, n])
-            return rr
-
-        def load_x(b):
-            xr = raw.tile([P, NT, D], BF16, name="xr", bufs=1)
-            nc.sync.dma_start(out=xr[:], in_=x[b].rearrange("(m n) d -> m n d", n=NT))
-            return xr
-
-        def turn(srcs, dst, use_scalar):
-            bank = ps_tr.tile([P, 4, P], F32, name="bank")
-            for i in range(2):
-                for u in range(2):
-                    nc.tensor.transpose(out=bank[:, 2 * i + u, :], in_=srcs[i][:, u::2], identity=ident[:])
-            o = dst.rearrange("p c t -> p (c t)").bitcast(F32).rearrange("p (i m u) -> p i m u", i=2, u=2)
-            s = bank[:].rearrange("p (i u) m -> p i m u", u=2)
-            if use_scalar:
-                nc.scalar.copy(out=o, in_=s)
-            else:
-                nc.vector.tensor_copy(out=o, in_=s)
-
-        def quantize(cd, sc, grp):
-            nc.vector.quantize_mx(out=cd.bitcast(FP8X4), scales=sc, in_=grp)
-
-        def words(ap):
-            return ap.bitcast(F32)
-
-        kc, ks, qc, qs, vc, vsc, xc, xs = {}, {}, {}, {}, {}, {}, {}, {}
-        rabt = {}
+        gains = const.tile([P, GS, P, 4], BF16)
+        ident = const.tile([P, P], F32)
+        neghalf = const.tile([P, 1], F32)
+        warm = const.tile([P, 1], F32)
+        wsc = const.tile([P, D], U8, align_bytes=64)
+        ww = codes.tile([P, GD, D], U32, name="ww", align_bytes=64)
+        kc, ks, qc, qs, vc, vsc, xc, xs, rabt = {}, {}, {}, {}, {}, {}, {}, {}, {}
         for h in range(H):
             rabt[h] = codes.tile([P, NT, GS, P, 4], BF16, name=f"rabt{h}", align_bytes=64)
         for b in range(B):
@@ -107,51 +118,143 @@ def tile_hstupointwisetransducer_d1p_kernel(tc, q, k, rab, c, v_bytes, v_scale, 
                 qs[b, h] = codes.tile([P, T], U8, name=f"qs{b}{h}", align_bytes=64)
                 vc[b, h] = codes.tile([P, GS, E], U32, name=f"vc{b}{h}", align_bytes=64)
                 vsc[b, h] = codes.tile([P, GS, E], U8, name=f"vsc{b}{h}", align_bytes=64)
-        ww = codes.tile([P, GD, D], U32, name="ww", align_bytes=64)
 
-        def prep_v(b, h, vb):
-            for g in range(GS):
-                grp = work.tile([P, 512, 4], BF16, name="grp", align_bytes=64, bufs=5)
-                wide = work.tile([P, 4, E], BF16, name="wide", bufs=2)
-                for t in range(4):
-                    for j in range(4):
-                        nc.scalar.activation(
-                            out=wide[:, t, P * j : P * (j + 1)], in_=vb[:, g, E * t + P * j : E * t + P * (j + 1)].bitcast(FP8),
-                            func=ACT.Copy, scale=vs[:, (b * H + h) * GS + g, 4 * t + j : 4 * t + j + 1],
-                        )
-                nc.vector.tensor_copy(
-                    out=grp[:].rearrange("p (f i) t -> p f t i", i=4), in_=wide[:].rearrange("p t (f i) -> p f t i", i=4)
+        rt = {}
+
+        def load(key):
+            kind = key[0]
+            if kind == "v":
+                b, h = key[1:]
+                rt[key] = raw.tile([P, GS, 4 * E], U8, name="vb", bufs=2)
+                nc.sync.dma_start(out=rt[key][:], in_=v_bytes[b, h].rearrange("(g p t) f -> p g (t f)", p=P, t=4))
+            elif kind == "k":
+                b, h, g = key[1:]
+                rt[key] = raw.tile([P, 4, E], BF16, name="kr", bufs=4)
+                src = k[b, h].rearrange("(g m t) e -> g m t e", m=P, t=4)[g]
+                parts = 2 if (b, h, g) == (0, 0, 0) else 1
+                for i in range(parts):
+                    ts = slice(4 // parts * i, 4 // parts * (i + 1))
+                    nc.sync.dma_start(out=rt[key][:, ts], in_=src[:, ts])
+            elif kind == "q":
+                b, h = key[1:]
+                rt[key] = raw.tile([P, NT, E], BF16, name="qr", bufs=2)
+                nc.sync.dma_start(out=rt[key][:], in_=q[b, h].rearrange("(m n) e -> m n e", n=NT))
+            elif kind == "r":
+                h, n = key[1:]
+                rt[key] = raw.tile([P, S], BF16, name="rr", bufs=4)
+                nc.sync.dma_start(out=rt[key][:], in_=rab[h].rearrange("(m n) s -> m n s", n=NT)[:, n])
+            elif kind == "x":
+                rt[key] = raw.tile([P, NT, D], BF16, name="xr", bufs=1)
+                nc.sync.dma_start(out=rt[key][:], in_=x[key[1]].rearrange("(m n) d -> m n d", n=NT))
+            else:
+                nc.sync.dma_start(
+                    out=ww[:].bitcast(I32),
+                    in_=wu_words.rearrange("g p n t -> g p (n t)").bitcast(I32).rearrange("g p n -> p g n"),
                 )
-                quantize(vc[b, h][:, g, :], vsc[b, h][:, g, :], grp[:].rearrange("p c t -> p (c t)"))
+                for qd in range(4):
+                    nc.sync.dma_start(
+                        out=wsc[32 * qd : 32 * qd + 8, :].bitcast(I32), in_=wu_scales[:, 4 * qd : 4 * qd + 4, :].bitcast(I32)
+                    )
 
-        def prep_k(b, h, g, kr):
-            grp = work.tile([P, 512, 4], BF16, name="grp", align_bytes=64, bufs=5)
-            w = words(kr[:])
-            for i in range(2):
-                turn([w[:, 2 * i, :], w[:, 2 * i + 1, :]], grp[:, 256 * i : 256 * (i + 1), :], True)
-            sl = slice(512 * g, 512 * (g + 1))
-            quantize(kc[b, h][:, sl], ks[b, h][:, sl], grp[:].rearrange("p c t -> p (c t)"))
+        LOADS = {
+            -1: [("k", 0, 0, 0), ("k", 0, 0, 1), ("q", 0, 0), ("r", 0, 0), ("v", 0, 0), ("r", 0, 1), ("k", 0, 1, 0),
+                 ("k", 0, 1, 1), ("r", 0, 2), ("q", 0, 1), ("r", 0, 3), ("v", 0, 1)],
+            0: [("r", 1, 0), ("x", 0), ("k", 1, 0, 0), ("k", 1, 0, 1)],
+            1: [("r", 1, 1), ("w",)],
+            2: [("r", 1, 2), ("q", 1, 0), ("k", 1, 1, 0)],
+            3: [("r", 1, 3), ("v", 1, 0), ("k", 1, 1, 1)],
+            4: [("q", 1, 1)],
+            5: [("v", 1, 1), ("x", 1)],
+        }
 
-        def prep_q(b, h, qr):
-            grp = work.tile([P, 512, 4], BF16, name="grp", align_bytes=64, bufs=5)
-            w = words(qr[:])
-            for i in range(2):
-                turn([w[:, 2 * i, :], w[:, 2 * i + 1, :]], grp[:, 256 * i : 256 * (i + 1), :], True)
-            quantize(qc[b, h][:], qs[b, h][:], grp[:].rearrange("p c t -> p (c t)"))
+        groups, banks, wides = {}, {}, {}
 
-        def prep_x(b, g, xr):
-            grp = work.tile([P, 512, 4], BF16, name="grp", align_bytes=64, bufs=5)
-            w = words(xr[:])
-            for i in range(2):
-                turn([w[:, n, 256 * g : 256 * (g + 1)] for n in (2 * i, 2 * i + 1)], grp[:, 256 * i : 256 * (i + 1), :], True)
-            quantize(xc[b][:, g, :], xs[b][:, g, :], grp[:].rearrange("p c t -> p (c t)"))
+        def group(key):
+            if key not in groups:
+                if key[0] == "v":
+                    groups[key] = work.tile([P, 512, 4], BF16, name="vg", align_bytes=64, bufs=2)
+                else:
+                    groups[key] = work.tile([P, 512, 4], BF16, name="grp", align_bytes=64, bufs=4)
+            return groups[key]
 
-        def prep_rab(h, n, rr):
-            w = words(rr[:])
-            turn([w[:, 256 * g : 256 * (g + 1)] for g in range(GS)], rabt[h][:, n].rearrange("p g m t -> p (g m) t"), h == 1)
+        def turn(job):
+            kind = job[0]
+            if kind == "k":
+                b, h, g, i = job[1:]
+                w = rt["k", b, h, g][:].bitcast(F32)
+                srcs = [w[:, 2 * i + j, :] for j in range(2)]
+            elif kind == "q":
+                b, h, i = job[1:]
+                w = rt["q", b, h][:].bitcast(F32)
+                srcs = [w[:, 2 * i + j, :] for j in range(2)]
+            elif kind == "x":
+                b, g, i = job[1:]
+                w = rt["x", b][:].bitcast(F32)
+                srcs = [w[:, 2 * i + j, 256 * g : 256 * (g + 1)] for j in range(2)]
+            else:
+                w = rt["r", job[1], job[2]][:].bitcast(F32)
+                srcs = [w[:, 256 * g : 256 * (g + 1)] for g in range(GS)]
+            bank = ps_tr.tile([P, 4, P], F32, name="bank")
+            for j in range(2):
+                for u in range(2):
+                    nc.tensor.transpose(out=bank[:, 2 * j + u, :], in_=srcs[j][:, u::2], identity=ident[:])
+            banks[job] = bank
 
-        def scores(b, h, n):
-            banks = []
+        def empty(job, on_vector=False):
+            if job[0] == "r":
+                dst = rabt[job[1]][:, job[2]].rearrange("p g m t -> p (g m) t")
+            else:
+                i = job[-1]
+                dst = group(job[:-1])[:, 256 * i : 256 * (i + 1), :]
+            o = dst.rearrange("p c t -> p (c t)").bitcast(F32).rearrange("p (j m u) -> p j m u", j=2, u=2)
+            s = banks[job][:].rearrange("p (j u) m -> p j m u", u=2)
+            if on_vector:
+                nc.vector.tensor_copy(out=o, in_=s)
+            else:
+                nc.scalar.copy(out=o, in_=s)
+
+        def widen(job):
+            b, h, g, i = job
+            if i == 0:
+                wides[b, h, g] = work.tile([P, 4, E], BF16, name="wide", bufs=3)
+            wide = wides[b, h, g]
+            vb = rt["v", b, h]
+            for t in (2 * i, 2 * i + 1):
+                for j in range(4):
+                    c0 = E * t + P * j
+                    nc.scalar.activation(
+                        out=wide[:, t, P * j : P * (j + 1)], in_=vb[:, g, c0 : c0 + P].bitcast(FP8),
+                        func=ACT.Copy, scale=vs[:, (b * H + h) * GS + g, 4 * t + j : 4 * t + j + 1],
+                    )
+
+        def merge(job):
+            grp = group(("v",) + job)
+            nc.vector.tensor_copy(
+                out=grp[:].rearrange("p (f i) t -> p f t i", i=4),
+                in_=wides[job][:].rearrange("p t (f i) -> p f t i", i=4),
+            )
+
+        def quantize(key):
+            kind = key[0]
+            grp = group(key)
+            if kind == "k":
+                b, h, g = key[1:]
+                cd, sc = kc[b, h][:, 512 * g : 512 * (g + 1)], ks[b, h][:, 512 * g : 512 * (g + 1)]
+            elif kind == "q":
+                b, h = key[1:]
+                cd, sc = qc[b, h][:], qs[b, h][:]
+            elif kind == "x":
+                b, g = key[1:]
+                cd, sc = xc[b][:, g, :], xs[b][:, g, :]
+            else:
+                b, h, g = key[1:]
+                cd, sc = vc[b, h][:, g, :], vsc[b, h][:, g, :]
+            nc.vector.quantize_mx(out=cd.bitcast(FP8X4), scales=sc, in_=grp[:].rearrange("p c t -> p (c t)"))
+
+        sbank, ltile, stile, atile, acodes, outs, gbank, gates, stats, ys = {}, {}, {}, {}, {}, {}, {}, {}, {}, {}
+
+        def scores(u):
+            b, h, n = u
             for g in range(GS):
                 sc = ps_sc.tile([P, 4, P], F32, name="sc")
                 for t in range(4):
@@ -165,32 +268,36 @@ def tile_hstupointwisetransducer_d1p_kernel(tc, q, k, rab, c, v_bytes, v_scale, 
                         start=True,
                         stop=True,
                     )
-                banks.append(sc)
-            return banks
+                sbank[u, g] = sc
 
-        def logits(b, h, n):
-            banks = scores(b, h, n)
-            l = work.tile([P, GS, P, 4], F32, name="l", bufs=2)
+        def logits(u):
+            b, h, n = u
+            ltile[u] = work.tile([P, GS, P, 4], F32, name="l", bufs=2)
             for g in range(GS):
                 nc.vector.scalar_tensor_tensor(
-                    out=l[:, g], in0=banks[g][:].rearrange("p t m -> p m t"), scalar=ISQ, in1=rabt[h][:, n, g],
+                    out=ltile[u][:, g], in0=sbank[u, g][:].rearrange("p t m -> p m t"), scalar=ISQ, in1=rabt[h][:, n, g],
                     op0=ALU.mult, op1=ALU.add,
                 )
-            s = work.tile([P, GS, P, 4], F32, name="s", bufs=3)
-            nc.scalar.activation(out=s[:], in_=l[:], func=ACT.Silu)
-            return s
 
-        def weights(b, h, n, s):
-            a = work.tile([P, GS, P, 4], BF16, name="a", align_bytes=64, bufs=3)
-            eng = nc.gpsimd if (h == 0 and n % 2 == 1) or (h == 1 and n == 1) else nc.vector
-            eng.tensor_tensor(out=a[:], in0=s[:], in1=gain[:].unsqueeze(2).to_broadcast([P, GS, P, 4]), op=ALU.mult)
-            ac = work.tile([P, GS * P], U32, name=f"ac{h}", align_bytes=64, bufs=5 - 2 * h)
-            asc = work.tile([P, GS * P], U8, name=f"asc{h}", align_bytes=64, bufs=5 - 2 * h)
-            quantize(ac[:], asc[:], a[:].rearrange("p g m t -> p (g m t)"))
-            made[b, h, n] = (ac, asc)
+        def activate(u):
+            stile[u] = work.tile([P, GS, P, 4], F32, name="s", bufs=2)
+            nc.scalar.activation(out=stile[u][:], in_=ltile[u][:], func=ACT.Silu)
 
-        def values(b, h, ac, asc):
-            o = ps_acc.tile([P, E], F32, name="acc")
+        def weigh(u, eng):
+            atile[u] = work.tile([P, GS, P, 4], BF16, name="a", align_bytes=64, bufs=2)
+            eng.tensor_tensor(out=atile[u][:], in0=stile[u][:], in1=gains[:], op=ALU.mult)
+
+        def encode(u):
+            h = u[1]
+            ac = work.tile([P, GS * P], U32, name=f"ac{h}", align_bytes=64, bufs=6 - 3 * h)
+            asc = work.tile([P, GS * P], U8, name=f"asc{h}", align_bytes=64, bufs=6 - 3 * h)
+            nc.vector.quantize_mx(out=ac[:].bitcast(FP8X4), scales=asc[:], in_=atile[u][:].rearrange("p g m t -> p (g m t)"))
+            acodes[u] = (ac, asc)
+
+        def values(u):
+            b, h, n = u
+            ac, asc = acodes[u]
+            o = ps_o.tile([P, E], F32, name="o")
             for g in range(GS):
                 nc.tensor.matmul_mx(
                     out=o[:],
@@ -201,12 +308,12 @@ def tile_hstupointwisetransducer_d1p_kernel(tc, q, k, rab, c, v_bytes, v_scale, 
                     start=(g == 0),
                     stop=(g == GS - 1),
                 )
-            return o
+            outs[u] = o
 
-        def gate(b, n):
-            u = work.tile([P, D], F32, name="u", bufs=3)
+        def gate_products(bn):
+            b, n = bn
             for f in range(2):
-                acc = ps_acc.tile([P, E], F32, name="acc")
+                acc = ps_ga.tile([P, E], F32, name="acc")
                 cols = slice(E * f, E * (f + 1))
                 for g in range(GD):
                     nc.tensor.matmul_mx(
@@ -218,91 +325,124 @@ def tile_hstupointwisetransducer_d1p_kernel(tc, q, k, rab, c, v_bytes, v_scale, 
                         start=(g == 0),
                         stop=(g == GD - 1),
                     )
-                nc.scalar.activation(out=u[:, cols], in_=acc[:], func=ACT.Silu)
-            return u
+                gbank[bn, f] = acc
 
-        def finish(b, n, outs, u):
+        def gate_silu(bn):
+            gates[bn] = work.tile([P, D], F32, name="u", bufs=3)
+            for f in range(2):
+                nc.scalar.activation(out=gates[bn][:, E * f : E * (f + 1)], in_=gbank[bn, f][:], func=ACT.Silu)
+
+        def norm_stats(bn):
+            b, n = bn
             st = work.tile([P, 2, 6], F32, name="st", bufs=3)
             for h in range(H):
-                nc.vector.bn_stats(out=st[:, h, :], in_=outs[h][:])
+                nc.vector.bn_stats(out=st[:, h, :], in_=outs[b, h, n][:])
             mv = work.tile([P, 2], F32, name="mv", bufs=3)
             nc.vector.bn_aggr(out=mv[:], in_=st[:].rearrange("p h s -> p (h s)"))
             ve = work.tile([P, 1], F32, name="ve", bufs=3)
             nc.gpsimd.tensor_scalar(out=ve[:], in0=mv[:, 1:2], scalar1=1.0, scalar2=EPS, op0=ALU.mult, op1=ALU.add)
             rs = work.tile([P, 1], F32, name="rs", bufs=3)
             nc.gpsimd.tensor_tensor(out=rs[:], in0=ve[:], in1=neghalf[:], op=ALU.pow)
-            y = work.tile([P, D], F32, name="y", bufs=2)
+            stats[bn] = (mv, rs)
+
+        def norm_gate(bn):
+            b, n = bn
+            ys[bn] = work.tile([P, D], F32, name="y", bufs=3)
             for h in range(H):
                 cols = slice(E * h, E * (h + 1))
                 nc.vector.scalar_tensor_tensor(
-                    out=y[:, cols], in0=outs[h][:], scalar=mv[:, 0:1], in1=u[:, cols], op0=ALU.subtract, op1=ALU.mult
-                )
-            z = work.tile([P, D], F32, name="z", bufs=2)
-            nc.gpsimd.tensor_scalar(out=z[:], in0=y[:], scalar1=rs[:], scalar2=0.0, op0=ALU.mult, op1=ALU.add)
-            nc.sync.dma_start(out=out[b].rearrange("(m n) d -> m n d", n=NT)[:, n], in_=z[:])
-
-        made = {}
-
-        def load_w():
-            nc.sync.dma_start(
-                out=ww[:].bitcast(I32),
-                in_=wu_words.rearrange("g p n t -> g p (n t)").bitcast(I32).rearrange("g p n -> p g n"),
-            )
-            for qd in range(4):
-                nc.sync.dma_start(
-                    out=wsc[32 * qd : 32 * qd + 8, :].bitcast(I32), in_=wu_scales[:, 4 * qd : 4 * qd + 4, :].bitcast(I32)
+                    out=ys[bn][:, cols], in0=outs[b, h, n][:], scalar=stats[bn][0][:, 0:1], in1=gates[bn][:, cols],
+                    op0=ALU.subtract, op1=ALU.mult,
                 )
 
-        steps = {0: [], 1: []}
-        for b in range(B):
-            for h in range(H):
-                steps[b].append(("vb", lambda b=b, h=h: load_v(b, h), lambda r, b=b, h=h: prep_v(b, h, r)))
-                for g in range(GS):
-                    steps[b].append(("kr", lambda b=b, h=h, g=g: load_k(b, h, g), lambda r, b=b, h=h, g=g: prep_k(b, h, g, r)))
-                steps[b].append(("qr", lambda b=b, h=h: load_q(b, h), lambda r, b=b, h=h: prep_q(b, h, r)))
-                if b == 0:
-                    for n in range(NT):
-                        steps[b].append(("rr", lambda h=h, n=n: load_rab(h, n), lambda r, h=h, n=n: prep_rab(h, n, r)))
-            steps[b].append(("xr", lambda b=b: load_x(b), lambda r, b=b: [prep_x(b, gg, r) for gg in range(GD)]))
-        order = steps[0] + steps[1]
-        room = {"vb": 3, "kr": 4, "qr": 2, "rr": 4, "xr": 1}
-        state = {"loaded": 0, "done": 0}
-        tiles = {}
+        def store(bn):
+            b, n = bn
+            dst = out[b].rearrange("(m n) d -> m n d", n=NT)[:, n]
+            y, rs = ys[bn], stats[bn][1]
+            if bn == (B - 1, NT - 1):
+                nc.scalar.activation(out=y[:, :E], in_=y[:, :E], func=ACT.Copy, scale=rs[:])
+                nc.sync.dma_start(out=dst[:, :E], in_=y[:, :E])
+                nc.vector.tensor_scalar(out=y[:, E:], in0=y[:, E:], scalar1=rs[:], scalar2=None, op0=ALU.mult)
+                nc.scalar.dma_start(out=dst[:, E:], in_=y[:, E:])
+            else:
+                nc.scalar.activation(out=y[:], in_=y[:], func=ACT.Copy, scale=rs[:])
+                nc.sync.dma_start(out=dst, in_=y[:])
 
-        def load_ahead():
-            while state["loaded"] < len(order) and room[order[state["loaded"]][0]] > 0:
-                kind, load, prep = order[state["loaded"]]
-                room[kind] -= 1
-                tiles[state["loaded"]] = load()
-                if state["loaded"] == len(steps[0]) - 1:
-                    load_w()
-                state["loaded"] += 1
-
-        def prepare(count):
-            for i in range(count):
-                if state["done"] < len(order):
-                    load_ahead()
-                    kind, load, prep = order[state["done"]]
-                    prep(tiles[state["done"]])
-                    room[kind] += 1
-                    state["done"] += 1
-            load_ahead()
-
-        def close(b, n):
-            finish(b, n, [values(b, h, *made[b, h, n]) for h in range(H)], gate(b, n))
+        make_identity(nc, ident[:])
+        nc.gpsimd.memset(neghalf[:], -0.5)
+        nc.gpsimd.memset(wsc[:].bitcast(I32), 0)
+        nc.scalar.activation(out=warm[:], in_=neghalf[:], func=ACT.Silu)
+        nc.scalar.dma_start(out=gain[:], in_=c.rearrange("(g p t) -> p g t", p=P, t=4))
+        nc.scalar.dma_start(out=vs[:], in_=v_scale.rearrange("b h (g p t) c -> p (b h g) (t c)", p=P, t=4))
 
         units = [(b, h, n) for b in range(B) for h in range(H) for n in range(NT)]
-        ahead = {(0, 0): [3, 2, 2, 2], (0, 1): [1, 1, 1, 1], (1, 0): [2, 1, 1, 1], (1, 1): [0, 0, 0, 0]}
-        prepare(8)
-        held = {}
-        for i in range(len(units) + 1):
-            if i < len(units):
-                held[units[i]] = logits(*units[i])
-            if i > 0:
-                b, h, n = units[i - 1]
-                weights(b, h, n, held[b, h, n])
-                if h == 1:
-                    close(b, n)
-            if i < len(units):
-                b, h, n = units[i]
-                prepare(ahead[b, h][n])
+        last = len(units) - 1
+
+        with tc.manual_schedule(engines={ENG.PE, ENG.Activation, ENG.DVE, ENG.Pool}):
+            for key in LOADS[-1]:
+                load(key)
+            nc.vector.tensor_copy(out=gains[:], in_=gain[:].unsqueeze(2).to_broadcast([P, GS, P, 4]))
+            first = k_jobs(0, 0) + q_jobs(0, 0) + [("r", 0, 0)]
+            ready = {3: [("k", 0, 0, 0)], 5: [("k", 0, 0, 1), ("q", 0, 0)]}
+            for j, job in enumerate(first):
+                turn(job)
+                empty(job, on_vector=(j % 2 == 1))
+                for key in ready.get(j, []):
+                    quantize(key)
+            scores(units[0])
+            for job in TURN[0][:2]:
+                turn(job)
+
+            waiting = None
+            for i in range(len(units) + 3):
+                here = units[i] if i <= last else None
+                prev = units[i - 1] if 1 <= i <= last + 1 else None
+                done = units[i - 2] if 2 <= i <= last + 2 and units[i - 2][1] == H - 1 else None
+                closed = (done[0], done[2]) if done else None
+                to_store, waiting = waiting, closed
+                for key in LOADS.get(i, []):
+                    load(key)
+                if done:
+                    values((done[0], 0, done[2]))
+                    values(done)
+                if here:
+                    logits(here)
+                for key in EARLY.get(i, []):
+                    quantize(key)
+                if here and i < last:
+                    scores(units[i + 1])
+                jobs = TURN.get(i, [])
+                for job in jobs[2:]:
+                    turn(job)
+                for job in jobs[:2]:
+                    empty(job)
+                if here:
+                    activate(here)
+                if to_store:
+                    store(to_store)
+                for bn in GATE.get(i, []):
+                    gate_products(bn)
+                for job in jobs[2:]:
+                    empty(job)
+                for job in WIDEN.get(i, []):
+                    widen(job)
+                for bn in GATE.get(i, []):
+                    gate_silu(bn)
+                for job in TURN.get(i + 1, [])[:2]:
+                    turn(job)
+                for job in MERGE.get(i, []):
+                    merge(job)
+                pool_gain = prev and i in GAIN_ON_POOL
+                if prev:
+                    weigh(prev, nc.gpsimd if pool_gain else nc.vector)
+                late = LATE.get(i, [])
+                if prev and i > last:
+                    encode(prev)
+                if closed:
+                    norm_stats(closed)
+                for key in late:
+                    quantize(key)
+                if closed:
+                    norm_gate(closed)
+                if prev and i <= last:
+                    encode(prev)

from contextlib import ExitStack

import concourse.mybir as mybir
from concourse.masks import make_identity

B, H, T, S, E = 2, 2, 512, 1024, 512
D = H * E
EPS = 1e-5
FLOPS = 2 * (2 * B * H * T * S * E + B * T * D * D)

F32 = mybir.dt.float32
BF16 = mybir.dt.bfloat16
U32 = mybir.dt.uint32
I32 = mybir.dt.int32
U8 = mybir.dt.uint8
FP8 = mybir.dt.float8_e4m3fn
FP8X4 = mybir.dt.float8_e4m3fn_x4
ALU = mybir.AluOpType
ACT = mybir.ActivationFunctionType
ENG = mybir.EngineType

P = 128
GS = S // 512
GD = D // 512
NT = T // P
ISQ = 1.0 / (E ** 0.5)


def k_jobs(b, h):
    return [("k", b, h, g, i) for g in range(GS) for i in range(2)]


def q_jobs(b, h):
    return [("q", b, h, i) for i in range(2)]


def x_jobs(b):
    return [("x", b, g, i) for g in range(GD) for i in range(2)]


def w_jobs(b, h):
    return [(b, h, g, i) for g in range(GS) for i in range(2)]


K01, Q01, X0, K10, Q10, K11, Q11, X1 = (
    k_jobs(0, 1), q_jobs(0, 1), x_jobs(0), k_jobs(1, 0), q_jobs(1, 0), k_jobs(1, 1), q_jobs(1, 1), x_jobs(1)
)
W00, W01, W10, W11 = w_jobs(0, 0), w_jobs(0, 1), w_jobs(1, 0), w_jobs(1, 1)

TURN = {
    0: [("r", 0, 1)] + K01[0:2],
    1: [("r", 0, 2)] + K01[2:4],
    2: [("r", 0, 3)] + Q01,
    3: [("r", 1, 0)] + X0[0:2],
    4: [("r", 1, 1)] + X0[2:4],
    5: [("r", 1, 2)] + K10[0:3],
    6: [("r", 1, 3)] + K10[3:4] + Q10,
    7: K11[0:1],
    8: K11[1:2],
    9: K11[2:4],
    10: Q11,
    11: X1[0:2],
    12: X1[2:4],
}
WIDEN = {
    0: W00[0:1], 1: W00[1:2], 2: W00[2:4], 3: W01[0:2], 4: W01[2:4],
    7: W10[0:1], 8: W10[1:2], 9: W10[2:3], 10: W10[3:4], 11: W11[0:2], 12: W11[2:4],
}
MERGE = {2: [(0, 0, 0)], 3: [(0, 0, 1)], 4: [(0, 1, 0)], 5: [(0, 1, 1)], 10: [(1, 0, 0)], 11: [(1, 0, 1)], 12: [(1, 1, 0)], 13: [(1, 1, 1)]}
EARLY = {3: [("q", 0, 1)], 5: [("x", 0, 1)], 13: [("x", 1, 1)], 7: [("k", 1, 0, 1), ("q", 1, 0)], 11: [("q", 1, 1)]}
LATE = {
    1: [("k", 0, 1, 0)],
    2: [("k", 0, 1, 1)],
    3: [("v", 0, 0, 0)],
    4: [("v", 0, 0, 1), ("x", 0, 0)],
    5: [("v", 0, 1, 0), ("v", 0, 1, 1)],
    6: [("k", 1, 0, 0)],
    9: [("k", 1, 1, 0)],
    10: [("k", 1, 1, 1)],
    11: [("v", 1, 0, 0)],
    12: [("v", 1, 0, 1), ("x", 1, 0)],
    13: [("v", 1, 1, 0), ("v", 1, 1, 1)],
}
GATE = {5: [(0, 0)], 6: [(0, 1)], 7: [(0, 2)], 8: [(0, 3)], 13: [(1, 0)], 14: [(1, 1)], 15: [(1, 2), (1, 3)]}
GAIN_ON_POOL = ()


def tile_hstupointwisetransducer_d1p_kernel(tc, q, k, rab, c, v_bytes, v_scale, x, wu_words, wu_scales, out):
    nc = tc.nc
    with ExitStack() as ctx:
        const = ctx.enter_context(tc.tile_pool(name="const", bufs=1))
        codes = ctx.enter_context(tc.tile_pool(name="codes", bufs=1))
        raw = ctx.enter_context(tc.tile_pool(name="raw", bufs=4))
        work = ctx.enter_context(tc.tile_pool(name="work", bufs=3))
        ps_tr = ctx.enter_context(tc.psum_pool(name="ps_tr", bufs=2))
        ps_sc = ctx.enter_context(tc.psum_pool(name="ps_sc", bufs=2))
        ps_o = ctx.enter_context(tc.psum_pool(name="ps_o", bufs=2))
        ps_ga = ctx.enter_context(tc.psum_pool(name="ps_ga", bufs=2))

        vs = const.tile([P, B * H * GS, 16], F32)
        gain = const.tile([P, GS, 4], BF16)
        gains = const.tile([P, GS, P, 4], BF16)
        ident = const.tile([P, P], F32)
        neghalf = const.tile([P, 1], F32)
        warm = const.tile([P, 1], F32)
        wsc = const.tile([P, D], U8, align_bytes=64)
        ww = codes.tile([P, GD, D], U32, name="ww", align_bytes=64)
        kc, ks, qc, qs, vc, vsc, xc, xs, rabt = {}, {}, {}, {}, {}, {}, {}, {}, {}
        for h in range(H):
            rabt[h] = codes.tile([P, NT, GS, P, 4], BF16, name=f"rabt{h}", align_bytes=64)
        for b in range(B):
            xc[b] = codes.tile([P, GD, T], U32, name=f"xc{b}", align_bytes=64)
            xs[b] = codes.tile([P, GD, T], U8, name=f"xs{b}", align_bytes=64)
            for h in range(H):
                kc[b, h] = codes.tile([P, S], U32, name=f"kc{b}{h}", align_bytes=64)
                ks[b, h] = codes.tile([P, S], U8, name=f"ks{b}{h}", align_bytes=64)
                qc[b, h] = codes.tile([P, T], U32, name=f"qc{b}{h}", align_bytes=64)
                qs[b, h] = codes.tile([P, T], U8, name=f"qs{b}{h}", align_bytes=64)
                vc[b, h] = codes.tile([P, GS, E], U32, name=f"vc{b}{h}", align_bytes=64)
                vsc[b, h] = codes.tile([P, GS, E], U8, name=f"vsc{b}{h}", align_bytes=64)

        rt = {}

        def load(key):
            kind = key[0]
            if kind == "v":
                b, h = key[1:]
                rt[key] = raw.tile([P, GS, 4 * E], U8, name="vb", bufs=2)
                nc.sync.dma_start(out=rt[key][:], in_=v_bytes[b, h].rearrange("(g p t) f -> p g (t f)", p=P, t=4))
            elif kind == "k":
                b, h, g = key[1:]
                rt[key] = raw.tile([P, 4, E], BF16, name="kr", bufs=4)
                src = k[b, h].rearrange("(g m t) e -> g m t e", m=P, t=4)[g]
                parts = 2 if (b, h, g) == (0, 0, 0) else 1
                for i in range(parts):
                    ts = slice(4 // parts * i, 4 // parts * (i + 1))
                    nc.sync.dma_start(out=rt[key][:, ts], in_=src[:, ts])
            elif kind == "q":
                b, h = key[1:]
                rt[key] = raw.tile([P, NT, E], BF16, name="qr", bufs=2)
                nc.sync.dma_start(out=rt[key][:], in_=q[b, h].rearrange("(m n) e -> m n e", n=NT))
            elif kind == "r":
                h, n = key[1:]
                rt[key] = raw.tile([P, S], BF16, name="rr", bufs=4)
                nc.sync.dma_start(out=rt[key][:], in_=rab[h].rearrange("(m n) s -> m n s", n=NT)[:, n])
            elif kind == "x":
                rt[key] = raw.tile([P, NT, D], BF16, name="xr", bufs=1)
                nc.sync.dma_start(out=rt[key][:], in_=x[key[1]].rearrange("(m n) d -> m n d", n=NT))
            else:
                nc.sync.dma_start(
                    out=ww[:].bitcast(I32),
                    in_=wu_words.rearrange("g p n t -> g p (n t)").bitcast(I32).rearrange("g p n -> p g n"),
                )
                for qd in range(4):
                    nc.sync.dma_start(
                        out=wsc[32 * qd : 32 * qd + 8, :].bitcast(I32), in_=wu_scales[:, 4 * qd : 4 * qd + 4, :].bitcast(I32)
                    )

        LOADS = {
            -1: [("k", 0, 0, 0), ("k", 0, 0, 1), ("q", 0, 0), ("r", 0, 0), ("v", 0, 0), ("r", 0, 1), ("k", 0, 1, 0),
                 ("k", 0, 1, 1), ("r", 0, 2), ("q", 0, 1), ("r", 0, 3), ("v", 0, 1)],
            0: [("r", 1, 0), ("x", 0), ("k", 1, 0, 0), ("k", 1, 0, 1)],
            1: [("r", 1, 1), ("w",)],
            2: [("r", 1, 2), ("q", 1, 0), ("k", 1, 1, 0)],
            3: [("r", 1, 3), ("v", 1, 0), ("k", 1, 1, 1)],
            4: [("q", 1, 1)],
            5: [("v", 1, 1), ("x", 1)],
        }

        groups, banks, wides = {}, {}, {}

        def group(key):
            if key not in groups:
                if key[0] == "v":
                    groups[key] = work.tile([P, 512, 4], BF16, name="vg", align_bytes=64, bufs=2)
                else:
                    groups[key] = work.tile([P, 512, 4], BF16, name="grp", align_bytes=64, bufs=4)
            return groups[key]

        def turn(job):
            kind = job[0]
            if kind == "k":
                b, h, g, i = job[1:]
                w = rt["k", b, h, g][:].bitcast(F32)
                srcs = [w[:, 2 * i + j, :] for j in range(2)]
            elif kind == "q":
                b, h, i = job[1:]
                w = rt["q", b, h][:].bitcast(F32)
                srcs = [w[:, 2 * i + j, :] for j in range(2)]
            elif kind == "x":
                b, g, i = job[1:]
                w = rt["x", b][:].bitcast(F32)
                srcs = [w[:, 2 * i + j, 256 * g : 256 * (g + 1)] for j in range(2)]
            else:
                w = rt["r", job[1], job[2]][:].bitcast(F32)
                srcs = [w[:, 256 * g : 256 * (g + 1)] for g in range(GS)]
            bank = ps_tr.tile([P, 4, P], F32, name="bank")
            for j in range(2):
                for u in range(2):
                    nc.tensor.transpose(out=bank[:, 2 * j + u, :], in_=srcs[j][:, u::2], identity=ident[:])
            banks[job] = bank

        def empty(job, on_vector=False):
            if job[0] == "r":
                dst = rabt[job[1]][:, job[2]].rearrange("p g m t -> p (g m) t")
            else:
                i = job[-1]
                dst = group(job[:-1])[:, 256 * i : 256 * (i + 1), :]
            o = dst.rearrange("p c t -> p (c t)").bitcast(F32).rearrange("p (j m u) -> p j m u", j=2, u=2)
            s = banks[job][:].rearrange("p (j u) m -> p j m u", u=2)
            if on_vector:
                nc.vector.tensor_copy(out=o, in_=s)
            else:
                nc.scalar.copy(out=o, in_=s)

        def widen(job):
            b, h, g, i = job
            if i == 0:
                wides[b, h, g] = work.tile([P, 4, E], BF16, name="wide", bufs=3)
            wide = wides[b, h, g]
            vb = rt["v", b, h]
            for t in (2 * i, 2 * i + 1):
                for j in range(4):
                    c0 = E * t + P * j
                    nc.scalar.activation(
                        out=wide[:, t, P * j : P * (j + 1)], in_=vb[:, g, c0 : c0 + P].bitcast(FP8),
                        func=ACT.Copy, scale=vs[:, (b * H + h) * GS + g, 4 * t + j : 4 * t + j + 1],
                    )

        def merge(job):
            grp = group(("v",) + job)
            nc.vector.tensor_copy(
                out=grp[:].rearrange("p (f i) t -> p f t i", i=4),
                in_=wides[job][:].rearrange("p t (f i) -> p f t i", i=4),
            )

        def quantize(key):
            kind = key[0]
            grp = group(key)
            if kind == "k":
                b, h, g = key[1:]
                cd, sc = kc[b, h][:, 512 * g : 512 * (g + 1)], ks[b, h][:, 512 * g : 512 * (g + 1)]
            elif kind == "q":
                b, h = key[1:]
                cd, sc = qc[b, h][:], qs[b, h][:]
            elif kind == "x":
                b, g = key[1:]
                cd, sc = xc[b][:, g, :], xs[b][:, g, :]
            else:
                b, h, g = key[1:]
                cd, sc = vc[b, h][:, g, :], vsc[b, h][:, g, :]
            nc.vector.quantize_mx(out=cd.bitcast(FP8X4), scales=sc, in_=grp[:].rearrange("p c t -> p (c t)"))

        sbank, ltile, stile, atile, acodes, outs, gbank, gates, stats, ys = {}, {}, {}, {}, {}, {}, {}, {}, {}, {}

        def scores(u):
            b, h, n = u
            for g in range(GS):
                sc = ps_sc.tile([P, 4, P], F32, name="sc")
                for t in range(4):
                    c0 = 512 * g + P * t
                    nc.tensor.matmul_mx(
                        out=sc[:, t, :],
                        lhsT=kc[b, h][:, c0 : c0 + P].bitcast(FP8X4),
                        lhsT_scale=ks[b, h][:, c0 : c0 + P],
                        rhs=qc[b, h][:, P * n : P * (n + 1)].bitcast(FP8X4),
                        rhs_scale=qs[b, h][:, P * n : P * (n + 1)],
                        start=True,
                        stop=True,
                    )
                sbank[u, g] = sc

        def logits(u):
            b, h, n = u
            ltile[u] = work.tile([P, GS, P, 4], F32, name="l", bufs=2)
            for g in range(GS):
                nc.vector.scalar_tensor_tensor(
                    out=ltile[u][:, g], in0=sbank[u, g][:].rearrange("p t m -> p m t"), scalar=ISQ, in1=rabt[h][:, n, g],
                    op0=ALU.mult, op1=ALU.add,
                )

        def activate(u):
            stile[u] = work.tile([P, GS, P, 4], F32, name="s", bufs=2)
            nc.scalar.activation(out=stile[u][:], in_=ltile[u][:], func=ACT.Silu)

        def weigh(u, eng):
            atile[u] = work.tile([P, GS, P, 4], BF16, name="a", align_bytes=64, bufs=2)
            eng.tensor_tensor(out=atile[u][:], in0=stile[u][:], in1=gains[:], op=ALU.mult)

        def encode(u):
            h = u[1]
            ac = work.tile([P, GS * P], U32, name=f"ac{h}", align_bytes=64, bufs=6 - 3 * h)
            asc = work.tile([P, GS * P], U8, name=f"asc{h}", align_bytes=64, bufs=6 - 3 * h)
            nc.vector.quantize_mx(out=ac[:].bitcast(FP8X4), scales=asc[:], in_=atile[u][:].rearrange("p g m t -> p (g m t)"))
            acodes[u] = (ac, asc)

        def values(u):
            b, h, n = u
            ac, asc = acodes[u]
            o = ps_o.tile([P, E], F32, name="o")
            for g in range(GS):
                nc.tensor.matmul_mx(
                    out=o[:],
                    lhsT=ac[:, P * g : P * (g + 1)].bitcast(FP8X4),
                    lhsT_scale=asc[:, P * g : P * (g + 1)],
                    rhs=vc[b, h][:, g, :].bitcast(FP8X4),
                    rhs_scale=vsc[b, h][:, g, :],
                    start=(g == 0),
                    stop=(g == GS - 1),
                )
            outs[u] = o

        def gate_products(bn):
            b, n = bn
            for f in range(2):
                acc = ps_ga.tile([P, E], F32, name="acc")
                cols = slice(E * f, E * (f + 1))
                for g in range(GD):
                    nc.tensor.matmul_mx(
                        out=acc[:],
                        lhsT=xc[b][:, g, P * n : P * (n + 1)].bitcast(FP8X4),
                        lhsT_scale=xs[b][:, g, P * n : P * (n + 1)],
                        rhs=ww[:, g, cols].bitcast(FP8X4),
                        rhs_scale=wsc[4 * g : P, cols],
                        start=(g == 0),
                        stop=(g == GD - 1),
                    )
                gbank[bn, f] = acc

        def gate_silu(bn):
            gates[bn] = work.tile([P, D], F32, name="u", bufs=3)
            for f in range(2):
                nc.scalar.activation(out=gates[bn][:, E * f : E * (f + 1)], in_=gbank[bn, f][:], func=ACT.Silu)

        def norm_stats(bn):
            b, n = bn
            st = work.tile([P, 2, 6], F32, name="st", bufs=3)
            for h in range(H):
                nc.vector.bn_stats(out=st[:, h, :], in_=outs[b, h, n][:])
            mv = work.tile([P, 2], F32, name="mv", bufs=3)
            nc.vector.bn_aggr(out=mv[:], in_=st[:].rearrange("p h s -> p (h s)"))
            ve = work.tile([P, 1], F32, name="ve", bufs=3)
            nc.gpsimd.tensor_scalar(out=ve[:], in0=mv[:, 1:2], scalar1=1.0, scalar2=EPS, op0=ALU.mult, op1=ALU.add)
            rs = work.tile([P, 1], F32, name="rs", bufs=3)
            nc.gpsimd.tensor_tensor(out=rs[:], in0=ve[:], in1=neghalf[:], op=ALU.pow)
            stats[bn] = (mv, rs)

        def norm_gate(bn):
            b, n = bn
            ys[bn] = work.tile([P, D], F32, name="y", bufs=3)
            for h in range(H):
                cols = slice(E * h, E * (h + 1))
                nc.vector.scalar_tensor_tensor(
                    out=ys[bn][:, cols], in0=outs[b, h, n][:], scalar=stats[bn][0][:, 0:1], in1=gates[bn][:, cols],
                    op0=ALU.subtract, op1=ALU.mult,
                )

        def store(bn):
            b, n = bn
            dst = out[b].rearrange("(m n) d -> m n d", n=NT)[:, n]
            y, rs = ys[bn], stats[bn][1]
            if bn == (B - 1, NT - 1):
                nc.scalar.activation(out=y[:, :E], in_=y[:, :E], func=ACT.Copy, scale=rs[:])
                nc.sync.dma_start(out=dst[:, :E], in_=y[:, :E])
                nc.vector.tensor_scalar(out=y[:, E:], in0=y[:, E:], scalar1=rs[:], scalar2=None, op0=ALU.mult)
                nc.scalar.dma_start(out=dst[:, E:], in_=y[:, E:])
            else:
                nc.scalar.activation(out=y[:], in_=y[:], func=ACT.Copy, scale=rs[:])
                nc.sync.dma_start(out=dst, in_=y[:])

        make_identity(nc, ident[:])
        nc.gpsimd.memset(neghalf[:], -0.5)
        nc.gpsimd.memset(wsc[:].bitcast(I32), 0)
        nc.scalar.activation(out=warm[:], in_=neghalf[:], func=ACT.Silu)
        nc.scalar.dma_start(out=gain[:], in_=c.rearrange("(g p t) -> p g t", p=P, t=4))
        nc.scalar.dma_start(out=vs[:], in_=v_scale.rearrange("b h (g p t) c -> p (b h g) (t c)", p=P, t=4))

        units = [(b, h, n) for b in range(B) for h in range(H) for n in range(NT)]
        last = len(units) - 1

        with tc.manual_schedule(engines={ENG.PE, ENG.Activation, ENG.DVE, ENG.Pool}):
            for key in LOADS[-1]:
                load(key)
            nc.vector.tensor_copy(out=gains[:], in_=gain[:].unsqueeze(2).to_broadcast([P, GS, P, 4]))
            first = k_jobs(0, 0) + q_jobs(0, 0) + [("r", 0, 0)]
            ready = {3: [("k", 0, 0, 0)], 5: [("k", 0, 0, 1), ("q", 0, 0)]}
            for j, job in enumerate(first):
                turn(job)
                empty(job, on_vector=(j % 2 == 1))
                for key in ready.get(j, []):
                    quantize(key)
            scores(units[0])
            for job in TURN[0][:2]:
                turn(job)

            waiting = None
            for i in range(len(units) + 3):
                here = units[i] if i <= last else None
                prev = units[i - 1] if 1 <= i <= last + 1 else None
                done = units[i - 2] if 2 <= i <= last + 2 and units[i - 2][1] == H - 1 else None
                closed = (done[0], done[2]) if done else None
                to_store, waiting = waiting, closed
                for key in LOADS.get(i, []):
                    load(key)
                if done:
                    values((done[0], 0, done[2]))
                    values(done)
                if here:
                    logits(here)
                for key in EARLY.get(i, []):
                    quantize(key)
                if here and i < last:
                    scores(units[i + 1])
                jobs = TURN.get(i, [])
                for job in jobs[2:]:
                    turn(job)
                for job in jobs[:2]:
                    empty(job)
                if here:
                    activate(here)
                if to_store:
                    store(to_store)
                for bn in GATE.get(i, []):
                    gate_products(bn)
                for job in jobs[2:]:
                    empty(job)
                for job in WIDEN.get(i, []):
                    widen(job)
                for bn in GATE.get(i, []):
                    gate_silu(bn)
                for job in TURN.get(i + 1, [])[:2]:
                    turn(job)
                for job in MERGE.get(i, []):
                    merge(job)
                pool_gain = prev and i in GAIN_ON_POOL
                if prev:
                    weigh(prev, nc.gpsimd if pool_gain else nc.vector)
                late = LATE.get(i, [])
                if prev and i > last:
                    encode(prev)
                if closed:
                    norm_stats(closed)
                for key in late:
                    quantize(key)
                if closed:
                    norm_gate(closed)
                if prev and i <= last:
                    encode(prev)
